import numpy as np
CORES = [0,8,16,24,32,40,48,56,128,136,144,152,160,168,176,184]
N = 16
ROOT = 12
WIDTHS = [3,8,13,18,23,28,4,9,14,19,24,29,5,10,15,20]
XW = 29
def setup_inputs(rng):
    return {"x": rng.standard_normal((N, 128, XW), dtype=np.float32)}
def reference(x):
    g = np.concatenate([x[r][:, :WIDTHS[r]] for r in range(N)], axis=1)
    y = np.full((N, 128, g.shape[1]), np.nan, x.dtype)
    y[ROOT] = g
    return {"y": y}

@@ -1,0 +1,62 @@
+SCRATCH = {
+    "land": ("sbuf", [128, 242], "float32"),
+}
+SEMAPHORES = ["loaded", "sent", "arrived", "stored"]
+
+
+def engines(mask):
+    return bin(mask).count("1")
+
+
+def plan(T, topo):
+    widths = T.tables["WIDTHS"]
+    root = T.cores[T.root]
+    via = [None] * len(widths)
+    load = {2: 0, 6: 0}
+    for r in sorted(range(len(widths)), key=lambda r: -widths[r]):
+        c = T.cores[r]
+        if c == root or topo.may_write(c, root):
+            continue
+        if topo.mates(c, root):
+            via[r] = c + 2
+            continue
+        k = 2 if load[2] <= load[6] else 6
+        load[k] += widths[r]
+        via[r] = c + k
+    return via
+
+
+def rank_program(g, core, T, topo):
+    widths = T.tables["WIDTHS"]
+    offs = [sum(widths[:r]) for r in range(len(widths))]
+    root = T.cores[T.root]
+    via = plan(T, topo)
+    rank = T.rank_of(core)
+
+    def send(r, dst):
+        sl = T.land[:, offs[r]:offs[r] + widths[r]]
+        rid, pid = topo.addr(dst, core)
+        m = topo.mask(core, dst)
+        g.remote_dma(sl, sl, T.sem.arrived, T.sem.sent, pid, rid, m)
+        g.wait_ge(T.sem.sent, engines(m))
+
+    if rank is None:
+        for r, f in enumerate(via):
+            if f == core:
+                g.wait_ge(T.sem.arrived, engines(topo.mask(T.cores[r], core)))
+                send(r, root)
+        return
+
+    w, o = widths[rank], offs[rank]
+    g.dma_start(T.land[:, o:o + w], T.x[:, 0:w]).then_inc(T.sem.loaded, 16)
+    g.wait_ge(T.sem.loaded, 16)
+    if core != root:
+        send(rank, root if via[rank] is None else via[rank])
+        return
+    total = 0
+    for r, c in enumerate(T.cores):
+        if c != root:
+            total += engines(topo.mask(c if via[r] is None else via[r], root))
+    g.wait_ge(T.sem.arrived, total)
+    g.dma_start(T.y[:, :], T.land[:, :]).then_inc(T.sem.stored, 16)
+    g.wait_ge(T.sem.stored, 16)

@@ -1,5 +1,13 @@
 SCRATCH = {
     "land": ("sbuf", [128, 242], "float32"),
+    "d8": ("dram", [128, 8], "float32"),
+    "d9": ("dram", [128, 9], "float32"),
+    "d10": ("dram", [128, 10], "float32"),
+    "d18": ("dram", [128, 18], "float32"),
+    "d19": ("dram", [128, 19], "float32"),
+    "d20": ("dram", [128, 20], "float32"),
+    "d28": ("dram", [128, 28], "float32"),
+    "d29": ("dram", [128, 29], "float32"),
 }
 SEMAPHORES = ["loaded", "sent", "arrived", "stored"]
 
@@ -32,26 +40,33 @@ def rank_program(g, core, T, topo):
     root = T.cores[T.root]
     via = plan(T, topo)
     rank = T.rank_of(core)
+    stage = {8: T.d8, 9: T.d9, 10: T.d10, 18: T.d18, 19: T.d19, 20: T.d20, 28: T.d28, 29: T.d29}
 
-    def send(r, dst):
-        sl = T.land[:, offs[r]:offs[r] + widths[r]]
+    def send(out, in_, dst):
         rid, pid = topo.addr(dst, core)
         m = topo.mask(core, dst)
-        g.remote_dma(sl, sl, T.sem.arrived, T.sem.sent, pid, rid, m)
+        g.remote_dma(out, in_, T.sem.arrived, T.sem.sent, pid, rid, m)
         g.wait_ge(T.sem.sent, engines(m))
 
     if rank is None:
         for r, f in enumerate(via):
             if f == core:
                 g.wait_ge(T.sem.arrived, engines(topo.mask(T.cores[r], core)))
-                send(r, root)
+                send(T.land[:, offs[r]:offs[r] + widths[r]], stage[widths[r]][:, :], root)
         return
 
     w, o = widths[rank], offs[rank]
-    g.dma_start(T.land[:, o:o + w], T.x[:, 0:w]).then_inc(T.sem.loaded, 16)
+    sl = T.land[:, o:o + w]
+    if via[rank] is not None:
+        d = stage[w]
+        g.dma_start(d[:, :], T.x[:, 0:w]).then_inc(T.sem.loaded, 16)
+        g.wait_ge(T.sem.loaded, 16)
+        send(d[:, :], d[:, :], via[rank])
+        return
+    g.dma_start(sl, T.x[:, 0:w]).then_inc(T.sem.loaded, 16)
     g.wait_ge(T.sem.loaded, 16)
     if core != root:
-        send(rank, root if via[rank] is None else via[rank])
+        send(sl, sl, root)
         return
     total = 0
     for r, c in enumerate(T.cores):

SCRATCH = {
    "land": ("sbuf", [128, 242], "float32"),
    "d8": ("dram", [128, 8], "float32"),
    "d9": ("dram", [128, 9], "float32"),
    "d10": ("dram", [128, 10], "float32"),
    "d18": ("dram", [128, 18], "float32"),
    "d19": ("dram", [128, 19], "float32"),
    "d20": ("dram", [128, 20], "float32"),
    "d28": ("dram", [128, 28], "float32"),
    "d29": ("dram", [128, 29], "float32"),
}
SEMAPHORES = ["loaded", "sent", "arrived", "stored"]


def engines(mask):
    return bin(mask).count("1")


def plan(T, topo):
    widths = T.tables["WIDTHS"]
    root = T.cores[T.root]
    via = [None] * len(widths)
    load = {2: 0, 6: 0}
    for r in sorted(range(len(widths)), key=lambda r: -widths[r]):
        c = T.cores[r]
        if c == root or topo.may_write(c, root):
            continue
        if topo.mates(c, root):
            via[r] = c + 2
            continue
        k = 2 if load[2] <= load[6] else 6
        load[k] += widths[r]
        via[r] = c + k
    return via


def rank_program(g, core, T, topo):
    widths = T.tables["WIDTHS"]
    offs = [sum(widths[:r]) for r in range(len(widths))]
    root = T.cores[T.root]
    via = plan(T, topo)
    rank = T.rank_of(core)
    stage = {8: T.d8, 9: T.d9, 10: T.d10, 18: T.d18, 19: T.d19, 20: T.d20, 28: T.d28, 29: T.d29}

    def send(out, in_, dst):
        rid, pid = topo.addr(dst, core)
        m = topo.mask(core, dst)
        g.remote_dma(out, in_, T.sem.arrived, T.sem.sent, pid, rid, m)
        g.wait_ge(T.sem.sent, engines(m))

    if rank is None:
        for r, f in enumerate(via):
            if f == core:
                g.wait_ge(T.sem.arrived, engines(topo.mask(T.cores[r], core)))
                send(T.land[:, offs[r]:offs[r] + widths[r]], stage[widths[r]][:, :], root)
        return

    w, o = widths[rank], offs[rank]
    sl = T.land[:, o:o + w]
    if via[rank] is not None:
        d = stage[w]
        g.dma_start(d[:, :], T.x[:, 0:w]).then_inc(T.sem.loaded, 16)
        g.wait_ge(T.sem.loaded, 16)
        send(d[:, :], d[:, :], via[rank])
        return
    g.dma_start(sl, T.x[:, 0:w]).then_inc(T.sem.loaded, 16)
    g.wait_ge(T.sem.loaded, 16)
    if core != root:
        send(sl, sl, root)
        return
    total = 0
    for r, c in enumerate(T.cores):
        if c != root:
            total += engines(topo.mask(c if via[r] is None else via[r], root))
    g.wait_ge(T.sem.arrived, total)
    g.dma_start(T.y[:, :], T.land[:, :]).then_inc(T.sem.stored, 16)
    g.wait_ge(T.sem.stored, 16)
